import numpy as np
import ml_dtypes


def mxq(x, axis, fmt="e4m3"):
    dtype, down = {"e4m3": (ml_dtypes.float8_e4m3fn, 7), "e5m2": (ml_dtypes.float8_e5m2, 14)}[fmt]
    v = np.moveaxis(np.asarray(x, np.float32).astype(ml_dtypes.bfloat16).astype(np.float64), axis, -1)
    blocks = v.reshape(v.shape[:-1] + (-1, 32))
    amax = np.abs(blocks).max(-1, keepdims=True)
    byte = np.maximum(np.where(amax > 0, np.frexp(amax)[1] - 1 + 127, 0) - down, 1)
    scale = np.exp2(byte - 127.0)
    codes = (blocks / scale).astype(np.float32).astype(dtype).astype(np.float64)
    return np.moveaxis((codes * scale).reshape(v.shape), -1, axis)


WIDE = False


def mx_kscale(k):
    if not WIDE:
        return np.ones(k)
    levels = np.array([10, -10, 5, -5, 0])
    if k % 512:
        return np.exp2(np.random.permutation(np.resize(levels, k // 32))).repeat(32)
    a = np.empty((k // 512, 16))
    for p in range(k // 512):
        a[p, :8] = np.random.permutation(np.resize(levels, 8))
        for g in range(8):
            far = levels[np.abs(levels - a[p, g]) >= 10]
            a[p, g + 8] = far[np.random.randint(len(far))]
    return np.exp2(a.ravel()).repeat(32)


def f64(x):
    return np.asarray(x).astype(np.float64)


def striped(idx):
    return np.tile(np.asarray(idx).reshape(-1, 16).T, (8, 1)).astype(np.uint16)


def unstriped(offs):
    return offs[:16].T.reshape(-1).astype(np.int64)


E2M1 = np.array([0.0, 0.5, 1.0, 1.5, 2.0, 3.0, 4.0, 6.0, -0.0, -0.5, -1.0, -1.5, -2.0, -3.0, -4.0, -6.0])


def pack_weight(w, fmt):
    k, n = w.shape
    w = f64(np.asarray(w, np.float32).astype(ml_dtypes.bfloat16)).reshape(k // 32, 32, n)
    amax = np.abs(w).max(1)
    if fmt == "e4m3":
        byte = np.frexp(amax)[1] - 1 + 127 - 7
    else:
        mant, ex = np.frexp(amax / 6.0)
        byte = np.where(mant > 0.5, ex, ex - 1) + 127
    byte = np.clip(np.where(amax > 0, byte, 1), 1, 254)
    scaled = (w * np.exp2(127.0 - byte)[:, None, :]).reshape(k, n).astype(np.float32)
    by_word = np.ascontiguousarray(scaled.reshape(k // 512, 128, 4, n).transpose(0, 1, 3, 2))
    if fmt == "e4m3":
        words = by_word.astype(ml_dtypes.float8_e4m3fn).view(np.uint8)
    else:
        c = by_word.astype(ml_dtypes.float4_e2m1fn).view(np.uint8) & 0xF
        words = (c[..., 0::2] | (c[..., 1::2] << 4)).reshape(k // 512, 128, 2 * n)
    return np.ascontiguousarray(words), np.ascontiguousarray(byte.astype(np.uint8).reshape(k // 512, 16, n))


def unpack_weight(words, scales, fmt):
    g, _, n = scales.shape
    words = np.ascontiguousarray(words).reshape(g, 128, n, -1)
    if fmt == "e4m3":
        vals = words.view(ml_dtypes.float8_e4m3fn).astype(np.float64)
    else:
        nib = np.empty((g, 128, n, 4), np.uint8)
        nib[..., 0::2] = words & 0xF
        nib[..., 1::2] = words >> 4
        vals = E2M1[nib]
    vals = vals * np.repeat(np.exp2(scales.astype(np.float64) - 127.0), 8, axis=1)[..., None]
    return vals.transpose(0, 1, 3, 2).reshape(g * 512, n)


D, E, T, I, G, U, Q = 512, 512, 4096, 1024, 64, 512, 128


def setup_inputs():
    n = np.random.standard_normal
    idx = np.random.permutation(T)[:I]
    idx2 = np.random.permutation(U)[:G]
    fd = mx_kscale(D)
    fe = mx_kscale(E)
    keysp = pack_weight(n((D, T)) / fd[:, None], "e2m1")
    valsp = pack_weight(n((E, T)) / fe[:, None], "e2m1")
    return {
        "query": (n((D, Q)) * 0.6 / np.sqrt(D) * fd[:, None]).astype(np.float32),
        "keys_words": keysp[0],
        "keys_scales": keysp[1],
        "ptab": (n((Q, U)) * 0.25).astype(np.float32),
        "gout": (n((E, Q)) * 1 / np.sqrt(E) * fe[:, None]).astype(np.float32),
        "vals_words": valsp[0],
        "vals_scales": valsp[1],
        "old": (0.5 * n((Q, U))).astype(np.float32),
        "offs": striped(idx),
        "offs2": striped(idx2),
    }


def reference(query, keys_words, keys_scales, ptab, gout, vals_words, vals_scales, old, offs, offs2):
    idx = unstriped(offs)
    idx2 = unstriped(offs2)
    keysu = unpack_weight(keys_words, keys_scales, "e2m1")
    valsu = unpack_weight(vals_words, vals_scales, "e2m1")
    queryq = mxq(f64(query), 0, "e4m3")
    keysidxg = keysu[:, idx]
    a = queryq.T @ keysidxg
    x1 = np.exp(a)
    goutq = mxq(f64(gout), 0, "e4m3")
    valsidxg = valsu[:, idx]
    c0 = goutq.T @ valsidxg
    s = x1.reshape(Q, G, I // G).sum(axis=2)
    m1 = (x1 * c0).reshape(Q, G, I // G).sum(axis=2) / s
    tp = np.exp(f64(ptab)[:, idx2])
    p = np.exp(np.log(s) * tp)
    z = np.sum(p, axis=1, keepdims=True)
    dz = np.sum(p * m1, axis=1, keepdims=True) / np.square(z) * (-1.0)
    dp = 1.0 / z * m1 + dz
    dtp = dp * p * np.log(s)
    gs = dtp * tp * 8.0
    gf = np.zeros((Q, U))
    gf[:, idx2] = gs
    y = f64(old) + gf
    return y

@@ -1,0 +1,189 @@
+from contextlib import ExitStack
+
+import concourse.mybir as mybir
+from concourse.masks import make_identity
+
+D, T, I, G, U, Q = 512, 4096, 1024, 64, 512, 128
+FLOPS = 2 * 2 * D * Q * I
+
+F32 = mybir.dt.float32
+BF16 = mybir.dt.bfloat16
+I32 = mybir.dt.int32
+U32 = mybir.dt.uint32
+U16 = mybir.dt.uint16
+U8 = mybir.dt.uint8
+FP8X4 = mybir.dt.float8_e4m3fn_x4
+FP4X4 = mybir.dt.float4_e2m1fn_x4
+ALU = mybir.AluOpType
+ACT = mybir.ActivationFunctionType
+AXIS = mybir.AxisListType
+
+P = 128
+PACK = 4
+HALF = 512
+HALVES = I // HALF
+PAGE = I // G
+ROWS = D // 32
+
+
+def tile_attend_bpagepower_kernel(
+    tc, query, keys_words, keys_scales, ptab, gout, vals_words, vals_scales, old, offs, offs2, out
+):
+    nc = tc.nc
+    with ExitStack() as ctx:
+        sb = ctx.enter_context(tc.tile_pool(name="sb", bufs=1))
+        ps = ctx.enter_context(tc.psum_pool(name="ps", bufs=1))
+
+        slots = sb.tile([P, I // 16], U16, name="slots")
+        pages = sb.tile([P, G // 16], U16, name="pages")
+        nc.sync.dma_start(slots[:], offs)
+
+        def load_scales(src, name, tag, queue):
+            win = sb.tile([P, T], U8, name=name, tag=tag, align_bytes=64)
+            nc.vector.memset(win[:].bitcast(I32), 0)
+            for b in range(4):
+                queue.dma_start(win[:].bitcast(I32)[32 * b : 32 * b + 4, :], src[0].bitcast(I32)[4 * b : 4 * b + 4, :])
+            return win
+
+        def load_words(src, name, tag):
+            win = sb.tile([P, T], U16, name=name, tag=tag, align_bytes=64)
+            nc.sync.dma_start(win[:].bitcast(I32), src[0].bitcast(I32))
+            return win
+
+        def load_rows(src, name, tag):
+            raw = sb.tile([P, PACK, Q], F32, name=name, tag=tag, align_bytes=64)
+            nc.sync.dma_start(raw[:], src.rearrange("(p j) w -> p j w", j=PACK))
+            return raw
+
+        def cast_rows(raw, name):
+            grouped = sb.tile([P, Q, PACK], BF16, name=name, align_bytes=64)
+            nc.scalar.copy(grouped[:], raw[:].rearrange("p j w -> p w j"))
+            return grouped
+
+        def quantize(grouped, name):
+            codes = sb.tile([P, Q], U32, name=name + "_codes", align_bytes=64)
+            scales = sb.tile([P, Q], U8, name=name + "_scales", align_bytes=64)
+            nc.vector.quantize_mx(codes[:].bitcast(FP8X4), scales[:], grouped[:].rearrange("p w j -> p (w j)"))
+            return codes, scales
+
+        def gather_scales(win, name):
+            plane = sb.tile([P, I], U8, name=name + "_plane", align_bytes=64)
+            nc.vector.tensor_copy(plane[:], win[:].indirect(slots[:]))
+            return plane
+
+        def gather_words(win, h, name):
+            words = sb.tile([P, HALF], U16, name=name, tag=name, align_bytes=64)
+            cols = HALF // 16
+            nc.vector.tensor_copy(words[:], win[:].indirect(slots[:, h * cols : (h + 1) * cols]))
+            return words
+
+        def product(rows, words, plane, h, name):
+            bank = ps.tile([P, HALF], F32, name=name)
+            nc.tensor.matmul_mx(
+                bank[:],
+                lhsT=rows[0][:].bitcast(FP8X4),
+                lhsT_scale=rows[1][:],
+                rhs=words[:].bitcast(FP4X4),
+                rhs_scale=plane[:, h * HALF : (h + 1) * HALF],
+                start=True,
+                stop=True,
+            )
+            return bank
+
+        kw_win = load_words(keys_words, "kw_win", "kw_win")
+        q_raw = load_rows(query, "q_raw", "rows_a")
+        g_raw = load_rows(gout, "g_raw", "rows_b")
+        nc.sync.dma_start(pages[:], offs2)
+        ptab_sb = sb.tile([P, U], F32, name="ptab_sb")
+        nc.sync.dma_start(ptab_sb[:], ptab)
+        ks_win = load_scales(keys_scales, "ks_win", "k_words1", nc.scalar)
+        vs_win = load_scales(vals_scales, "vs_win", "vs_win", nc.sync)
+
+        gf = sb.tile([P, U], F32, name="gf")
+        nc.vector.memset(gf[:], 0.0)
+        ident = sb.tile([P, P], F32, name="ident")
+        make_identity(nc, ident[:])
+
+        q_bf = cast_rows(q_raw, "q_bf")
+        g_bf = cast_rows(g_raw, "g_bf")
+        vw_win = load_words(vals_words, "vw_win", "rows_a")
+        old_sb = sb.tile([P, U], F32, name="old_sb", tag="rows_b", align_bytes=64)
+        nc.sync.dma_start(old_sb[:], old)
+
+        k_words = [gather_words(kw_win, 0, "k_words0")]
+        k_plane = gather_scales(ks_win, "k")
+        k_words.append(gather_words(kw_win, 1, "k_words1"))
+        q_mx = quantize(q_bf, "q")
+        g_mx = quantize(g_bf, "g")
+        logp = sb.tile([P, G], F32, name="logp")
+        nc.vector.tensor_copy(logp[:], ptab_sb[:].indirect(pages[:]))
+        powers = sb.tile([P, 2, G], F32, name="powers")
+        nc.scalar.activation(powers[:, 0, :], logp[:], ACT.Exp)
+        nc.scalar.activation(powers[:, 1, :], powers[:, 0, :], ACT.Copy, bias=-1.0)
+
+        x1 = []
+        quads = ps.tile([P, HALVES, P], F32, name="quads")
+        for h in range(HALVES):
+            a = product(q_mx, k_words[h], k_plane, h, "a%d" % h)
+            x = sb.tile([P, PACK, P], F32, name="x%d" % h)
+            nc.scalar.activation(x[:], a[:].rearrange("p (c t) -> p t c", t=PACK), ACT.Exp)
+            x1.append(x)
+            turned = ps.tile([P, P], F32, name="turned%d" % h)
+            for t in range(PACK):
+                nc.tensor.matmul(
+                    turned[:], lhsT=x[:, t, :], rhs=ident[:], is_transpose=True, start=(t == 0), stop=(t == PACK - 1)
+                )
+            turned_sb = sb.tile([P, P], F32, name="turned_sb%d" % h, tag=("turned_sb0", "v_words0")[h], align_bytes=64)
+            nc.scalar.copy(turned_sb[:], turned[:])
+            nc.tensor.transpose(quads[:, h, :], turned_sb[:], ident[:])
+
+        v_plane = gather_scales(vs_win, "v")
+
+        s = sb.tile([P, G], F32, name="s", tag="vs_win", align_bytes=64)
+        nc.vector.tensor_reduce(s[:], quads[:].rearrange("p h (g j) -> p (h g) j", j=PACK), AXIS.X, ALU.add)
+        ln_s = sb.tile([P, G], F32, name="ln_s")
+        nc.scalar.activation(ln_s[:], s[:], ACT.Ln)
+
+        v_words = [gather_words(vw_win, h, "v_words%d" % h) for h in range(HALVES)]
+        c0 = [product(g_mx, v_words[h], v_plane, h, "c%d" % h) for h in range(HALVES)]
+
+        expo = sb.tile([P, 2, G], F32, name="expo", tag="v_words0", align_bytes=64)
+        nc.vector.tensor_tensor(expo[:], powers[:], ln_s[:].unsqueeze(1).to_broadcast([P, 2, G]), ALU.mult)
+        neg_max = sb.tile([P, 1], F32, name="neg_max")
+        nc.vector.tensor_reduce(neg_max[:], expo[:, 0, :], AXIS.X, ALU.max, negate=True)
+        part = sb.tile([P, G], F32, name="part")
+        z = sb.tile([P, 1], F32, name="z")
+        nc.scalar.activation(part[:], expo[:, 0, :], ACT.Exp, bias=neg_max[:], accum_out=z[:])
+        part_s = sb.tile([P, G], F32, name="part_s")
+        nc.scalar.activation(part_s[:], expo[:, 1, :], ACT.Exp, bias=neg_max[:])
+
+        num = sb.tile([P, G], F32, name="num")
+        for h in range(HALVES):
+            c = c0[h]
+            xc = sb.tile([P, PACK, P], F32, name="xc%d" % h)
+            nc.vector.tensor_tensor(xc[:], c[:].rearrange("p (c t) -> p t c", t=PACK), x1[h][:], ALU.mult)
+            gh = G // HALVES
+            nc.vector.tensor_reduce(
+                num[:, h * gh : (h + 1) * gh], xc[:].rearrange("p t (g j) -> p g t j", j=PACK), AXIS.XY, ALU.add
+            )
+
+        rz = sb.tile([P, 1], F32, name="rz")
+        nc.vector.reciprocal(rz[:], z[:])
+        share = sb.tile([P, G], F32, name="share")
+        nc.vector.tensor_scalar(share[:], part[:], rz[:], None, ALU.mult)
+        factor = sb.tile([P, G], F32, name="factor")
+        nc.vector.tensor_scalar(factor[:], expo[:, 0, :], rz[:], -8.0, ALU.mult, ALU.mult)
+
+        wm = sb.tile([P, G], F32, name="wm")
+        total = sb.tile([P, 1], F32, name="total")
+        nc.vector.scalar_tensor_tensor(wm[:], num[:], 1.0, part_s[:], ALU.mult, ALU.mult, accum_out=total[:])
+        diff = sb.tile([P, G], F32, name="diff")
+        nc.vector.scalar_tensor_tensor(diff[:], share[:], total[:], wm[:], ALU.mult, ALU.subtract)
+        nc.vector.tensor_tensor(gf[:].indirect(pages[:]), diff[:], factor[:], ALU.mult)
+
+        half = U // 2
+        for h, queue in enumerate((nc.sync, nc.scalar)):
+            cols = slice(h * half, (h + 1) * half)
+            res = sb.tile([P, half], F32, name="res%d" % h)
+            nc.vector.tensor_tensor(res[:], gf[:, cols], old_sb[:, cols], ALU.add)
+            queue.dma_start(out[:, cols], res[:])

@@ -32,57 +32,41 @@ def tile_attend_bpagepower_kernel(
     nc = tc.nc
     with ExitStack() as ctx:
         sb = ctx.enter_context(tc.tile_pool(name="sb", bufs=1))
+        shared = ctx.enter_context(tc.tile_pool(name="shared", bufs=1))
         ps = ctx.enter_context(tc.psum_pool(name="ps", bufs=1))
 
         slots = sb.tile([P, I // 16], U16, name="slots")
         pages = sb.tile([P, G // 16], U16, name="pages")
         nc.sync.dma_start(slots[:], offs)
 
-        def load_scales(src, name, tag, queue):
-            win = sb.tile([P, T], U8, name=name, tag=tag, align_bytes=64)
-            nc.vector.memset(win[:].bitcast(I32), 0)
-            for b in range(4):
-                queue.dma_start(win[:].bitcast(I32)[32 * b : 32 * b + 4, :], src[0].bitcast(I32)[4 * b : 4 * b + 4, :])
-            return win
+        def load_scales(win, src):
+            nc.scalar.dma_start(win[:].bitcast(I32)[0:P:8, :], src[0].bitcast(I32))
 
-        def load_words(src, name, tag):
-            win = sb.tile([P, T], U16, name=name, tag=tag, align_bytes=64)
+        def load_words(win, src):
             nc.sync.dma_start(win[:].bitcast(I32), src[0].bitcast(I32))
-            return win
 
-        def load_rows(src, name, tag):
-            raw = sb.tile([P, PACK, Q], F32, name=name, tag=tag, align_bytes=64)
+        def load_rows(raw, src):
             nc.sync.dma_start(raw[:], src.rearrange("(p j) w -> p j w", j=PACK))
-            return raw
 
-        def cast_rows(raw, name):
-            grouped = sb.tile([P, Q, PACK], BF16, name=name, align_bytes=64)
-            nc.scalar.copy(grouped[:], raw[:].rearrange("p j w -> p w j"))
-            return grouped
+        def cast_rows(grouped, raw):
+            nc.scalar.copy(grouped, raw[:].rearrange("p j w -> p w j"))
 
-        def quantize(grouped, name):
-            codes = sb.tile([P, Q], U32, name=name + "_codes", align_bytes=64)
-            scales = sb.tile([P, Q], U8, name=name + "_scales", align_bytes=64)
-            nc.vector.quantize_mx(codes[:].bitcast(FP8X4), scales[:], grouped[:].rearrange("p w j -> p (w j)"))
-            return codes, scales
+        def gather_scales(plane, picked, win, queue):
+            nc.vector.tensor_copy(picked[:], win[:].indirect(slots[:]))
+            for b in range(0, P, 32):
+                queue.dma_start(plane[:].bitcast(I32)[b : b + 4, :], picked[:].bitcast(I32)[b : b + 32 : 8, :])
 
-        def gather_scales(win, name):
-            plane = sb.tile([P, I], U8, name=name + "_plane", align_bytes=64)
-            nc.vector.tensor_copy(plane[:], win[:].indirect(slots[:]))
-            return plane
-
-        def gather_words(win, h, name):
-            words = sb.tile([P, HALF], U16, name=name, tag=name, align_bytes=64)
+        def gather_words(words, win, h):
             cols = HALF // 16
             nc.vector.tensor_copy(words[:], win[:].indirect(slots[:, h * cols : (h + 1) * cols]))
             return words
 
         def product(rows, words, plane, h, name):
-            bank = ps.tile([P, HALF], F32, name=name)
+            bank = ps.tile([P, HALF], F32, name=name, tag=name)
             nc.tensor.matmul_mx(
                 bank[:],
-                lhsT=rows[0][:].bitcast(FP8X4),
-                lhsT_scale=rows[1][:],
+                lhsT=rows[0].bitcast(FP8X4),
+                lhsT_scale=rows[1],
                 rhs=words[:].bitcast(FP4X4),
                 rhs_scale=plane[:, h * HALF : (h + 1) * HALF],
                 start=True,
@@ -90,39 +74,58 @@ def tile_attend_bpagepower_kernel(
             )
             return bank
 
-        kw_win = load_words(keys_words, "kw_win", "kw_win")
-        q_raw = load_rows(query, "q_raw", "rows_a")
-        g_raw = load_rows(gout, "g_raw", "rows_b")
+        kw_win = shared.tile([P, T], U16, name="kw_win", offset=17408, align_bytes=64)
+        q_raw = shared.tile([P, PACK, Q], F32, name="q_raw", offset=T, align_bytes=64)
+        g_raw = sb.tile([P, PACK, Q], F32, name="g_raw")
+        ptab_sb = shared.tile([P, U], F32, name="ptab_sb", offset=13312, align_bytes=64)
+        load_words(kw_win, keys_words)
+        load_rows(q_raw, query)
+        load_rows(g_raw, gout)
         nc.sync.dma_start(pages[:], offs2)
-        ptab_sb = sb.tile([P, U], F32, name="ptab_sb")
         nc.sync.dma_start(ptab_sb[:], ptab)
-        ks_win = load_scales(keys_scales, "ks_win", "k_words1", nc.scalar)
-        vs_win = load_scales(vals_scales, "vs_win", "vs_win", nc.sync)
+
+        ks_win = shared.tile([P, T], U8, name="ks_win", offset=0, align_bytes=64)
+        ks_zero = ks_win[:].bitcast(I32)
+        nc.gpsimd.memset(ks_zero[:, 0 : T // 8], 0)
+        nc.vector.memset(ks_zero[:, T // 8 : T // 4], 0)
+        load_scales(ks_win, keys_scales)
+        vs_win = sb.tile([P, T], U8, name="vs_win", tag="vs_win", align_bytes=64)
+        nc.vector.memset(vs_win[:].bitcast(I32), 0)
+        load_scales(vs_win, vals_scales)
 
         gf = sb.tile([P, U], F32, name="gf")
         nc.vector.memset(gf[:], 0.0)
         ident = sb.tile([P, P], F32, name="ident")
         make_identity(nc, ident[:])
 
-        q_bf = cast_rows(q_raw, "q_bf")
-        g_bf = cast_rows(g_raw, "g_bf")
-        vw_win = load_words(vals_words, "vw_win", "rows_a")
-        old_sb = sb.tile([P, U], F32, name="old_sb", tag="rows_b", align_bytes=64)
-        nc.sync.dma_start(old_sb[:], old)
+        rows_bf = shared.tile([P, 2, Q, PACK], BF16, name="rows_bf", offset=15360, align_bytes=64)
+        cast_rows(rows_bf[:, 0], q_raw)
+        vw_win = shared.tile([P, T], U16, name="vw_win", offset=T, align_bytes=64)
+        load_words(vw_win, vals_words)
+        cast_rows(rows_bf[:, 1], g_raw)
+        k_plane = sb.tile([P, I], U8, name="k_plane", align_bytes=64)
+        k_picked = sb.tile([P, I], U8, name="k_picked", align_bytes=64)
+        gather_scales(k_plane, k_picked, ks_win, nc.sync)
 
-        k_words = [gather_words(kw_win, 0, "k_words0")]
-        k_plane = gather_scales(ks_win, "k")
-        k_words.append(gather_words(kw_win, 1, "k_words1"))
-        q_mx = quantize(q_bf, "q")
-        g_mx = quantize(g_bf, "g")
-        logp = sb.tile([P, G], F32, name="logp")
+        k_words = [
+            shared.tile([P, HALF], U16, name="k_words%d" % h, offset=2 * HALF * h, align_bytes=64)
+            for h in range(HALVES)
+        ]
+        codes = shared.tile([P, 2 * Q], U32, name="codes", offset=13312, align_bytes=64)
+        scales = shared.tile([P, 2 * Q], U8, name="scales", offset=14336, align_bytes=64)
+        logp = shared.tile([P, G], F32, name="logp", offset=2 * I, align_bytes=64)
+        gather_words(k_words[0], kw_win, 0)
         nc.vector.tensor_copy(logp[:], ptab_sb[:].indirect(pages[:]))
+        nc.vector.quantize_mx(codes[:].bitcast(FP8X4), scales[:], rows_bf[:].rearrange("p a w j -> p (a w j)"))
+        q_mx = (codes[:, 0:Q], scales[:, 0:Q])
+        g_mx = (codes[:, Q : 2 * Q], scales[:, Q : 2 * Q])
+        gather_words(k_words[1], kw_win, 1)
         powers = sb.tile([P, 2, G], F32, name="powers")
         nc.scalar.activation(powers[:, 0, :], logp[:], ACT.Exp)
         nc.scalar.activation(powers[:, 1, :], powers[:, 0, :], ACT.Copy, bias=-1.0)
 
         x1 = []
-        quads = ps.tile([P, HALVES, P], F32, name="quads")
+        quads = ps.tile([P, HALVES, P], F32, name="quads", tag="c0")
         for h in range(HALVES):
             a = product(q_mx, k_words[h], k_plane, h, "a%d" % h)
             x = sb.tile([P, PACK, P], F32, name="x%d" % h)
@@ -133,21 +136,28 @@ def tile_attend_bpagepower_kernel(
                 nc.tensor.matmul(
                     turned[:], lhsT=x[:, t, :], rhs=ident[:], is_transpose=True, start=(t == 0), stop=(t == PACK - 1)
                 )
-            turned_sb = sb.tile([P, P], F32, name="turned_sb%d" % h, tag=("turned_sb0", "v_words0")[h], align_bytes=64)
+            turned_sb = sb.tile([P, P], F32, name="turned_sb%d" % h, tag=("turned_sb0", "v_words1")[h], align_bytes=64)
             nc.scalar.copy(turned_sb[:], turned[:])
             nc.tensor.transpose(quads[:, h, :], turned_sb[:], ident[:])
 
-        v_plane = gather_scales(vs_win, "v")
+        v_plane = sb.tile([P, I], U8, name="v_plane", align_bytes=64)
+        v_picked = shared.tile([P, I], U8, name="v_picked", offset=16896, align_bytes=64)
+        gather_scales(v_plane, v_picked, vs_win, nc.sync)
+        old_sb = sb.tile([P, U], F32, name="old_sb", tag="vs_win", align_bytes=64)
+        nc.sync.dma_start(old_sb[:], old)
+        v_words = [sb.tile([P, HALF], U16, name="v_words0", tag="v_words0", align_bytes=64)]
+        gather_words(v_words[0], vw_win, 0)
 
-        s = sb.tile([P, G], F32, name="s", tag="vs_win", align_bytes=64)
+        s = sb.tile([P, G], F32, name="s")
         nc.vector.tensor_reduce(s[:], quads[:].rearrange("p h (g j) -> p (h g) j", j=PACK), AXIS.X, ALU.add)
         ln_s = sb.tile([P, G], F32, name="ln_s")
         nc.scalar.activation(ln_s[:], s[:], ACT.Ln)
 
-        v_words = [gather_words(vw_win, h, "v_words%d" % h) for h in range(HALVES)]
+        v_words.append(sb.tile([P, HALF], U16, name="v_words1", tag="v_words1", align_bytes=64))
+        gather_words(v_words[1], vw_win, 1)
         c0 = [product(g_mx, v_words[h], v_plane, h, "c%d" % h) for h in range(HALVES)]
 
-        expo = sb.tile([P, 2, G], F32, name="expo", tag="v_words0", align_bytes=64)
+        expo = shared.tile([P, 2, G], F32, name="expo", offset=T, align_bytes=64)
         nc.vector.tensor_tensor(expo[:], powers[:], ln_s[:].unsqueeze(1).to_broadcast([P, 2, G]), ALU.mult)
         neg_max = sb.tile([P, 1], F32, name="neg_max")
         nc.vector.tensor_reduce(neg_max[:], expo[:, 0, :], AXIS.X, ALU.max, negate=True)

@@ -32,31 +32,39 @@ def tile_attend_bpagepower_kernel(
     nc = tc.nc
     with ExitStack() as ctx:
         sb = ctx.enter_context(tc.tile_pool(name="sb", bufs=1))
-        shared = ctx.enter_context(tc.tile_pool(name="shared", bufs=1))
         ps = ctx.enter_context(tc.psum_pool(name="ps", bufs=1))
 
         slots = sb.tile([P, I // 16], U16, name="slots")
         pages = sb.tile([P, G // 16], U16, name="pages")
         nc.sync.dma_start(slots[:], offs)
 
-        def load_scales(win, src):
-            nc.scalar.dma_start(win[:].bitcast(I32)[0:P:8, :], src[0].bitcast(I32))
+        def load_scales(src, name, tag, queue):
+            win = sb.tile([P, T], U8, name=name, tag=tag, align_bytes=64)
+            nc.vector.memset(win[:].bitcast(I32), 0)
+            for b in range(4):
+                queue.dma_start(win[:].bitcast(I32)[32 * b : 32 * b + 4, :], src[0].bitcast(I32)[4 * b : 4 * b + 4, :])
+            return win
 
-        def load_words(win, src):
+        def load_words(src, name, tag):
+            win = sb.tile([P, T], U16, name=name, tag=tag, align_bytes=64)
             nc.sync.dma_start(win[:].bitcast(I32), src[0].bitcast(I32))
+            return win
 
-        def load_rows(raw, src):
+        def load_rows(src, name, tag):
+            raw = sb.tile([P, PACK, Q], F32, name=name, tag=tag, align_bytes=64)
             nc.sync.dma_start(raw[:], src.rearrange("(p j) w -> p j w", j=PACK))
+            return raw
 
         def cast_rows(grouped, raw):
             nc.scalar.copy(grouped, raw[:].rearrange("p j w -> p w j"))
 
-        def gather_scales(plane, picked, win, queue):
-            nc.vector.tensor_copy(picked[:], win[:].indirect(slots[:]))
-            for b in range(0, P, 32):
-                queue.dma_start(plane[:].bitcast(I32)[b : b + 4, :], picked[:].bitcast(I32)[b : b + 32 : 8, :])
+        def gather_scales(win, name, tag):
+            plane = sb.tile([P, I], U8, name=name, tag=tag, align_bytes=64)
+            nc.vector.tensor_copy(plane[:], win[:].indirect(slots[:]))
+            return plane
 
-        def gather_words(words, win, h):
+        def gather_words(win, h, name):
+            words = sb.tile([P, HALF], U16, name=name, tag=name, align_bytes=64)
             cols = HALF // 16
             nc.vector.tensor_copy(words[:], win[:].indirect(slots[:, h * cols : (h + 1) * cols]))
             return words
@@ -74,58 +82,42 @@ def tile_attend_bpagepower_kernel(
             )
             return bank
 
-        kw_win = shared.tile([P, T], U16, name="kw_win", offset=17408, align_bytes=64)
-        q_raw = shared.tile([P, PACK, Q], F32, name="q_raw", offset=T, align_bytes=64)
-        g_raw = sb.tile([P, PACK, Q], F32, name="g_raw")
-        ptab_sb = shared.tile([P, U], F32, name="ptab_sb", offset=13312, align_bytes=64)
-        load_words(kw_win, keys_words)
-        load_rows(q_raw, query)
-        load_rows(g_raw, gout)
+        kw_win = load_words(keys_words, "kw_win", "kw_win")
+        q_raw = load_rows(query, "q_raw", "rows_a")
+        g_raw = load_rows(gout, "g_raw", "rows_b")
         nc.sync.dma_start(pages[:], offs2)
-        nc.sync.dma_start(ptab_sb[:], ptab)
-
-        ks_win = shared.tile([P, T], U8, name="ks_win", offset=0, align_bytes=64)
-        ks_zero = ks_win[:].bitcast(I32)
-        nc.gpsimd.memset(ks_zero[:, 0 : T // 8], 0)
-        nc.vector.memset(ks_zero[:, T // 8 : T // 4], 0)
-        load_scales(ks_win, keys_scales)
-        vs_win = sb.tile([P, T], U8, name="vs_win", tag="vs_win", align_bytes=64)
-        nc.vector.memset(vs_win[:].bitcast(I32), 0)
-        load_scales(vs_win, vals_scales)
+        ks_win = load_scales(keys_scales, "ks_win", "ks_win", nc.sync)
+        vs_win = load_scales(vals_scales, "vs_win", "vs_win", nc.sync)
 
         gf = sb.tile([P, U], F32, name="gf")
         nc.vector.memset(gf[:], 0.0)
         ident = sb.tile([P, P], F32, name="ident")
         make_identity(nc, ident[:])
 
-        rows_bf = shared.tile([P, 2, Q, PACK], BF16, name="rows_bf", offset=15360, align_bytes=64)
+        rows_bf = sb.tile([P, 2, Q, PACK], BF16, name="rows_bf", align_bytes=64)
         cast_rows(rows_bf[:, 0], q_raw)
-        vw_win = shared.tile([P, T], U16, name="vw_win", offset=T, align_bytes=64)
-        load_words(vw_win, vals_words)
         cast_rows(rows_bf[:, 1], g_raw)
-        k_plane = sb.tile([P, I], U8, name="k_plane", align_bytes=64)
-        k_picked = sb.tile([P, I], U8, name="k_picked", align_bytes=64)
-        gather_scales(k_plane, k_picked, ks_win, nc.sync)
+        ptab_sb = sb.tile([P, U], F32, name="ptab_sb", tag="rows_a", align_bytes=64)
+        nc.sync.dma_start(ptab_sb[:], ptab)
+        vw_win = load_words(vals_words, "vw_win", "rows_b")
 
-        k_words = [
-            shared.tile([P, HALF], U16, name="k_words%d" % h, offset=2 * HALF * h, align_bytes=64)
-            for h in range(HALVES)
-        ]
-        codes = shared.tile([P, 2 * Q], U32, name="codes", offset=13312, align_bytes=64)
-        scales = shared.tile([P, 2 * Q], U8, name="scales", offset=14336, align_bytes=64)
-        logp = shared.tile([P, G], F32, name="logp", offset=2 * I, align_bytes=64)
-        gather_words(k_words[0], kw_win, 0)
-        nc.vector.tensor_copy(logp[:], ptab_sb[:].indirect(pages[:]))
+        k_words = [gather_words(kw_win, h, "k_words%d" % h) for h in range(HALVES)]
+        codes = sb.tile([P, 2 * Q], U32, name="codes", align_bytes=64)
+        scales = sb.tile([P, 2 * Q], U8, name="scales", align_bytes=64)
         nc.vector.quantize_mx(codes[:].bitcast(FP8X4), scales[:], rows_bf[:].rearrange("p a w j -> p (a w j)"))
         q_mx = (codes[:, 0:Q], scales[:, 0:Q])
         g_mx = (codes[:, Q : 2 * Q], scales[:, Q : 2 * Q])
-        gather_words(k_words[1], kw_win, 1)
+        k_plane = gather_scales(ks_win, "k_plane", "k_plane")
+        old_sb = sb.tile([P, U], F32, name="old_sb", tag="ks_win", align_bytes=64)
+        nc.sync.dma_start(old_sb[:], old)
+        logp = sb.tile([P, G], F32, name="logp")
+        nc.vector.tensor_copy(logp[:], ptab_sb[:].indirect(pages[:]))
         powers = sb.tile([P, 2, G], F32, name="powers")
         nc.scalar.activation(powers[:, 0, :], logp[:], ACT.Exp)
         nc.scalar.activation(powers[:, 1, :], powers[:, 0, :], ACT.Copy, bias=-1.0)
 
         x1 = []
-        quads = ps.tile([P, HALVES, P], F32, name="quads", tag="c0")
+        quads = ps.tile([P, HALVES, P], F32, name="quads")
         for h in range(HALVES):
             a = product(q_mx, k_words[h], k_plane, h, "a%d" % h)
             x = sb.tile([P, PACK, P], F32, name="x%d" % h)
@@ -136,28 +128,21 @@ def tile_attend_bpagepower_kernel(
                 nc.tensor.matmul(
                     turned[:], lhsT=x[:, t, :], rhs=ident[:], is_transpose=True, start=(t == 0), stop=(t == PACK - 1)
                 )
-            turned_sb = sb.tile([P, P], F32, name="turned_sb%d" % h, tag=("turned_sb0", "v_words1")[h], align_bytes=64)
+            turned_sb = sb.tile([P, P], F32, name="turned_sb%d" % h)
             nc.scalar.copy(turned_sb[:], turned[:])
             nc.tensor.transpose(quads[:, h, :], turned_sb[:], ident[:])
 
-        v_plane = sb.tile([P, I], U8, name="v_plane", align_bytes=64)
-        v_picked = shared.tile([P, I], U8, name="v_picked", offset=16896, align_bytes=64)
-        gather_scales(v_plane, v_picked, vs_win, nc.sync)
-        old_sb = sb.tile([P, U], F32, name="old_sb", tag="vs_win", align_bytes=64)
-        nc.sync.dma_start(old_sb[:], old)
-        v_words = [sb.tile([P, HALF], U16, name="v_words0", tag="v_words0", align_bytes=64)]
-        gather_words(v_words[0], vw_win, 0)
+        v_plane = gather_scales(vs_win, "v_plane", "rows_a")
+        v_words = [gather_words(vw_win, h, "v_words%d" % h) for h in range(HALVES)]
+        c0 = [product(g_mx, v_words[h], v_plane, h, "c%d" % h) for h in range(HALVES)]
 
-        s = sb.tile([P, G], F32, name="s")
+        s = sb.tile([P, G], F32, name="s", tag="v_words0", align_bytes=64)
         nc.vector.tensor_reduce(s[:], quads[:].rearrange("p h (g j) -> p (h g) j", j=PACK), AXIS.X, ALU.add)
         ln_s = sb.tile([P, G], F32, name="ln_s")
         nc.scalar.activation(ln_s[:], s[:], ACT.Ln)
 
-        v_words.append(sb.tile([P, HALF], U16, name="v_words1", tag="v_words1", align_bytes=64))
-        gather_words(v_words[1], vw_win, 1)
-        c0 = [product(g_mx, v_words[h], v_plane, h, "c%d" % h) for h in range(HALVES)]
 
-        expo = shared.tile([P, 2, G], F32, name="expo", offset=T, align_bytes=64)
+        expo = sb.tile([P, 2, G], F32, name="expo")
         nc.vector.tensor_tensor(expo[:], powers[:], ln_s[:].unsqueeze(1).to_broadcast([P, 2, G]), ALU.mult)
         neg_max = sb.tile([P, 1], F32, name="neg_max")
         nc.vector.tensor_reduce(neg_max[:], expo[:, 0, :], AXIS.X, ALU.max, negate=True)
@@ -167,33 +152,28 @@ def tile_attend_bpagepower_kernel(
         part_s = sb.tile([P, G], F32, name="part_s")
         nc.scalar.activation(part_s[:], expo[:, 1, :], ACT.Exp, bias=neg_max[:])
 
-        num = sb.tile([P, G], F32, name="num")
+        xc = sb.tile([P, PACK, HALVES * P], F32, name="xc")
         for h in range(HALVES):
-            c = c0[h]
-            xc = sb.tile([P, PACK, P], F32, name="xc%d" % h)
-            nc.vector.tensor_tensor(xc[:], c[:].rearrange("p (c t) -> p t c", t=PACK), x1[h][:], ALU.mult)
-            gh = G // HALVES
-            nc.vector.tensor_reduce(
-                num[:, h * gh : (h + 1) * gh], xc[:].rearrange("p t (g j) -> p g t j", j=PACK), AXIS.XY, ALU.add
+            nc.vector.tensor_tensor(
+                xc[:, :, h * P : (h + 1) * P], c0[h][:].rearrange("p (c t) -> p t c", t=PACK), x1[h][:], ALU.mult
             )
-
         rz = sb.tile([P, 1], F32, name="rz")
         nc.vector.reciprocal(rz[:], z[:])
         share = sb.tile([P, G], F32, name="share")
-        nc.vector.tensor_scalar(share[:], part[:], rz[:], None, ALU.mult)
-        factor = sb.tile([P, G], F32, name="factor")
-        nc.vector.tensor_scalar(factor[:], expo[:, 0, :], rz[:], -8.0, ALU.mult, ALU.mult)
+        nc.scalar.activation(share[:], part[:], ACT.Copy, scale=rz[:])
+        num = sb.tile([P, G], F32, name="num")
+        nc.vector.tensor_reduce(num[:], xc[:].rearrange("p t (g j) -> p g t j", j=PACK), AXIS.XY, ALU.add)
 
         wm = sb.tile([P, G], F32, name="wm")
         total = sb.tile([P, 1], F32, name="total")
-        nc.vector.scalar_tensor_tensor(wm[:], num[:], 1.0, part_s[:], ALU.mult, ALU.mult, accum_out=total[:])
+        nc.vector.scalar_tensor_tensor(wm[:], num[:], -8.0, part_s[:], ALU.mult, ALU.mult, accum_out=total[:])
         diff = sb.tile([P, G], F32, name="diff")
         nc.vector.scalar_tensor_tensor(diff[:], share[:], total[:], wm[:], ALU.mult, ALU.subtract)
-        nc.vector.tensor_tensor(gf[:].indirect(pages[:]), diff[:], factor[:], ALU.mult)
+        nc.vector.tensor_tensor(gf[:].indirect(pages[:]), diff[:], expo[:, 0, :], ALU.mult)
 
         half = U // 2
         for h, queue in enumerate((nc.sync, nc.scalar)):
             cols = slice(h * half, (h + 1) * half)
             res = sb.tile([P, half], F32, name="res%d" % h)
-            nc.vector.tensor_tensor(res[:], gf[:, cols], old_sb[:, cols], ALU.add)
+            nc.vector.scalar_tensor_tensor(res[:], gf[:, cols], rz[:], old_sb[:, cols], ALU.mult, ALU.add)
             queue.dma_start(out[:, cols], res[:])

from contextlib import ExitStack

import concourse.mybir as mybir
from concourse.masks import make_identity

D, T, I, G, U, Q = 512, 4096, 1024, 64, 512, 128
FLOPS = 2 * 2 * D * Q * I

F32 = mybir.dt.float32
BF16 = mybir.dt.bfloat16
I32 = mybir.dt.int32
U32 = mybir.dt.uint32
U16 = mybir.dt.uint16
U8 = mybir.dt.uint8
FP8X4 = mybir.dt.float8_e4m3fn_x4
FP4X4 = mybir.dt.float4_e2m1fn_x4
ALU = mybir.AluOpType
ACT = mybir.ActivationFunctionType
AXIS = mybir.AxisListType

P = 128
PACK = 4
HALF = 512
HALVES = I // HALF
PAGE = I // G
ROWS = D // 32


def tile_attend_bpagepower_kernel(
    tc, query, keys_words, keys_scales, ptab, gout, vals_words, vals_scales, old, offs, offs2, out
):
    nc = tc.nc
    with ExitStack() as ctx:
        sb = ctx.enter_context(tc.tile_pool(name="sb", bufs=1))
        ps = ctx.enter_context(tc.psum_pool(name="ps", bufs=1))

        slots = sb.tile([P, I // 16], U16, name="slots")
        pages = sb.tile([P, G // 16], U16, name="pages")
        nc.sync.dma_start(slots[:], offs)

        def load_scales(src, name, tag, queue):
            win = sb.tile([P, T], U8, name=name, tag=tag, align_bytes=64)
            nc.vector.memset(win[:].bitcast(I32), 0)
            for b in range(4):
                queue.dma_start(win[:].bitcast(I32)[32 * b : 32 * b + 4, :], src[0].bitcast(I32)[4 * b : 4 * b + 4, :])
            return win

        def load_words(src, name, tag):
            win = sb.tile([P, T], U16, name=name, tag=tag, align_bytes=64)
            nc.sync.dma_start(win[:].bitcast(I32), src[0].bitcast(I32))
            return win

        def load_rows(src, name, tag):
            raw = sb.tile([P, PACK, Q], F32, name=name, tag=tag, align_bytes=64)
            nc.sync.dma_start(raw[:], src.rearrange("(p j) w -> p j w", j=PACK))
            return raw

        def cast_rows(grouped, raw):
            nc.scalar.copy(grouped, raw[:].rearrange("p j w -> p w j"))

        def gather_scales(win, name, tag):
            plane = sb.tile([P, I], U8, name=name, tag=tag, align_bytes=64)
            nc.vector.tensor_copy(plane[:], win[:].indirect(slots[:]))
            return plane

        def gather_words(win, h, name):
            words = sb.tile([P, HALF], U16, name=name, tag=name, align_bytes=64)
            cols = HALF // 16
            nc.vector.tensor_copy(words[:], win[:].indirect(slots[:, h * cols : (h + 1) * cols]))
            return words

        def product(rows, words, plane, h, name):
            bank = ps.tile([P, HALF], F32, name=name, tag=name)
            nc.tensor.matmul_mx(
                bank[:],
                lhsT=rows[0].bitcast(FP8X4),
                lhsT_scale=rows[1],
                rhs=words[:].bitcast(FP4X4),
                rhs_scale=plane[:, h * HALF : (h + 1) * HALF],
                start=True,
                stop=True,
            )
            return bank

        kw_win = load_words(keys_words, "kw_win", "kw_win")
        q_raw = load_rows(query, "q_raw", "rows_a")
        g_raw = load_rows(gout, "g_raw", "rows_b")
        nc.sync.dma_start(pages[:], offs2)
        ks_win = load_scales(keys_scales, "ks_win", "ks_win", nc.sync)
        vs_win = load_scales(vals_scales, "vs_win", "vs_win", nc.sync)

        gf = sb.tile([P, U], F32, name="gf")
        nc.vector.memset(gf[:], 0.0)
        ident = sb.tile([P, P], F32, name="ident")
        make_identity(nc, ident[:])

        rows_bf = sb.tile([P, 2, Q, PACK], BF16, name="rows_bf", align_bytes=64)
        cast_rows(rows_bf[:, 0], q_raw)
        cast_rows(rows_bf[:, 1], g_raw)
        ptab_sb = sb.tile([P, U], F32, name="ptab_sb", tag="rows_a", align_bytes=64)
        nc.sync.dma_start(ptab_sb[:], ptab)
        vw_win = load_words(vals_words, "vw_win", "rows_b")

        k_words = [gather_words(kw_win, h, "k_words%d" % h) for h in range(HALVES)]
        codes = sb.tile([P, 2 * Q], U32, name="codes", align_bytes=64)
        scales = sb.tile([P, 2 * Q], U8, name="scales", align_bytes=64)
        nc.vector.quantize_mx(codes[:].bitcast(FP8X4), scales[:], rows_bf[:].rearrange("p a w j -> p (a w j)"))
        q_mx = (codes[:, 0:Q], scales[:, 0:Q])
        g_mx = (codes[:, Q : 2 * Q], scales[:, Q : 2 * Q])
        k_plane = gather_scales(ks_win, "k_plane", "k_plane")
        old_sb = sb.tile([P, U], F32, name="old_sb", tag="ks_win", align_bytes=64)
        nc.sync.dma_start(old_sb[:], old)
        logp = sb.tile([P, G], F32, name="logp")
        nc.vector.tensor_copy(logp[:], ptab_sb[:].indirect(pages[:]))
        powers = sb.tile([P, 2, G], F32, name="powers")
        nc.scalar.activation(powers[:, 0, :], logp[:], ACT.Exp)
        nc.scalar.activation(powers[:, 1, :], powers[:, 0, :], ACT.Copy, bias=-1.0)

        x1 = []
        quads = ps.tile([P, HALVES, P], F32, name="quads")
        for h in range(HALVES):
            a = product(q_mx, k_words[h], k_plane, h, "a%d" % h)
            x = sb.tile([P, PACK, P], F32, name="x%d" % h)
            nc.scalar.activation(x[:], a[:].rearrange("p (c t) -> p t c", t=PACK), ACT.Exp)
            x1.append(x)
            turned = ps.tile([P, P], F32, name="turned%d" % h)
            for t in range(PACK):
                nc.tensor.matmul(
                    turned[:], lhsT=x[:, t, :], rhs=ident[:], is_transpose=True, start=(t == 0), stop=(t == PACK - 1)
                )
            turned_sb = sb.tile([P, P], F32, name="turned_sb%d" % h)
            nc.scalar.copy(turned_sb[:], turned[:])
            nc.tensor.transpose(quads[:, h, :], turned_sb[:], ident[:])

        v_plane = gather_scales(vs_win, "v_plane", "rows_a")
        v_words = [gather_words(vw_win, h, "v_words%d" % h) for h in range(HALVES)]
        c0 = [product(g_mx, v_words[h], v_plane, h, "c%d" % h) for h in range(HALVES)]

        s = sb.tile([P, G], F32, name="s", tag="v_words0", align_bytes=64)
        nc.vector.tensor_reduce(s[:], quads[:].rearrange("p h (g j) -> p (h g) j", j=PACK), AXIS.X, ALU.add)
        ln_s = sb.tile([P, G], F32, name="ln_s")
        nc.scalar.activation(ln_s[:], s[:], ACT.Ln)


        expo = sb.tile([P, 2, G], F32, name="expo")
        nc.vector.tensor_tensor(expo[:], powers[:], ln_s[:].unsqueeze(1).to_broadcast([P, 2, G]), ALU.mult)
        neg_max = sb.tile([P, 1], F32, name="neg_max")
        nc.vector.tensor_reduce(neg_max[:], expo[:, 0, :], AXIS.X, ALU.max, negate=True)
        part = sb.tile([P, G], F32, name="part")
        z = sb.tile([P, 1], F32, name="z")
        nc.scalar.activation(part[:], expo[:, 0, :], ACT.Exp, bias=neg_max[:], accum_out=z[:])
        part_s = sb.tile([P, G], F32, name="part_s")
        nc.scalar.activation(part_s[:], expo[:, 1, :], ACT.Exp, bias=neg_max[:])

        xc = sb.tile([P, PACK, HALVES * P], F32, name="xc")
        for h in range(HALVES):
            nc.vector.tensor_tensor(
                xc[:, :, h * P : (h + 1) * P], c0[h][:].rearrange("p (c t) -> p t c", t=PACK), x1[h][:], ALU.mult
            )
        rz = sb.tile([P, 1], F32, name="rz")
        nc.vector.reciprocal(rz[:], z[:])
        share = sb.tile([P, G], F32, name="share")
        nc.scalar.activation(share[:], part[:], ACT.Copy, scale=rz[:])
        num = sb.tile([P, G], F32, name="num")
        nc.vector.tensor_reduce(num[:], xc[:].rearrange("p t (g j) -> p g t j", j=PACK), AXIS.XY, ALU.add)

        wm = sb.tile([P, G], F32, name="wm")
        total = sb.tile([P, 1], F32, name="total")
        nc.vector.scalar_tensor_tensor(wm[:], num[:], -8.0, part_s[:], ALU.mult, ALU.mult, accum_out=total[:])
        diff = sb.tile([P, G], F32, name="diff")
        nc.vector.scalar_tensor_tensor(diff[:], share[:], total[:], wm[:], ALU.mult, ALU.subtract)
        nc.vector.tensor_tensor(gf[:].indirect(pages[:]), diff[:], expo[:, 0, :], ALU.mult)

        half = U // 2
        for h, queue in enumerate((nc.sync, nc.scalar)):
            cols = slice(h * half, (h + 1) * half)
            res = sb.tile([P, half], F32, name="res%d" % h)
            nc.vector.scalar_tensor_tensor(res[:], gf[:, cols], rz[:], old_sb[:, cols], ALU.mult, ALU.add)
            queue.dma_start(out[:, cols], res[:])
